import numpy as np
import ml_dtypes


def mxq(x, axis, fmt="e4m3"):
    dtype, down = {"e4m3": (ml_dtypes.float8_e4m3fn, 7), "e5m2": (ml_dtypes.float8_e5m2, 14)}[fmt]
    v = np.moveaxis(np.asarray(x, np.float32).astype(ml_dtypes.bfloat16).astype(np.float64), axis, -1)
    blocks = v.reshape(v.shape[:-1] + (-1, 32))
    amax = np.abs(blocks).max(-1, keepdims=True)
    byte = np.maximum(np.where(amax > 0, np.frexp(amax)[1] - 1 + 127, 0) - down, 1)
    scale = np.exp2(byte - 127.0)
    codes = (blocks / scale).astype(np.float32).astype(dtype).astype(np.float64)
    return np.moveaxis((codes * scale).reshape(v.shape), -1, axis)


WIDE = False


def mx_kscale(k):
    if not WIDE:
        return np.ones(k)
    levels = np.array([10, -10, 5, -5, 0])
    if k % 512:
        return np.exp2(np.random.permutation(np.resize(levels, k // 32))).repeat(32)
    a = np.empty((k // 512, 16))
    for p in range(k // 512):
        a[p, :8] = np.random.permutation(np.resize(levels, 8))
        for g in range(8):
            far = levels[np.abs(levels - a[p, g]) >= 10]
            a[p, g + 8] = far[np.random.randint(len(far))]
    return np.exp2(a.ravel()).repeat(32)


def f64(x):
    return np.asarray(x).astype(np.float64)


def striped(idx):
    return np.tile(idx.reshape(-1, 16).T, (8, 1)).astype(np.uint16)


def unstriped(offs):
    return offs[:16].T.reshape(-1).astype(np.int64)


def pack_weight(w):
    k, n = w.shape
    w = f64(np.asarray(w, np.float32).astype(ml_dtypes.bfloat16)).reshape(k // 32, 32, n)
    amax = np.abs(w).max(1)
    byte = np.clip(np.where(amax > 0, np.frexp(amax)[1] - 1 + 127 - 7, 1), 1, 254)
    scaled = (w * np.exp2(127.0 - byte)[:, None, :]).reshape(k, n).astype(np.float32)
    words = np.ascontiguousarray(scaled.reshape(k // 512, 128, 4, n).transpose(0, 1, 3, 2)).astype(ml_dtypes.float8_e4m3fn).view(np.uint8)
    return words, np.ascontiguousarray(byte.astype(np.uint8).reshape(k // 512, 16, n))


def unpack_weight(words, scales):
    g, p, n, _ = words.shape
    vals = np.ascontiguousarray(words).view(ml_dtypes.float8_e4m3fn).astype(np.float64) * np.repeat(np.exp2(scales.astype(np.float64) - 127.0), 8, axis=1)[..., None]
    return vals.transpose(0, 1, 3, 2).reshape(g * 512, n)


E2M1 = np.array([0.0, 0.5, 1.0, 1.5, 2.0, 3.0, 4.0, 6.0, -0.0, -0.5, -1.0, -1.5, -2.0, -3.0, -4.0, -6.0])


def pack_fp4(w):
    k, n = w.shape
    w = f64(np.asarray(w, np.float32).astype(ml_dtypes.bfloat16)).reshape(k // 32, 32, n)
    amax = np.abs(w).max(1)
    mant, ex = np.frexp(amax / 6.0)
    byte = np.clip(np.where(amax > 0, np.where(mant > 0.5, ex, ex - 1) + 127, 1), 1, 254)
    scaled = (w * np.exp2(127.0 - byte)[:, None, :]).reshape(k, n).astype(np.float32)
    c = np.ascontiguousarray(scaled.reshape(k // 512, 128, 4, n).transpose(0, 1, 3, 2)).astype(ml_dtypes.float4_e2m1fn).view(np.uint8) & 0xF
    words = (c[..., 0::2] | (c[..., 1::2] << 4)).reshape(k // 512, 128, 2 * n)
    return np.ascontiguousarray(words), np.ascontiguousarray(byte.astype(np.uint8).reshape(k // 512, 16, n))


def unpack_fp4(words, scales):
    g, _, n = scales.shape
    words = np.ascontiguousarray(words).reshape(g, 128, n, 2)
    nib = np.empty((g, 128, n, 4), np.uint8)
    nib[..., 0::2] = words & 0xF
    nib[..., 1::2] = words >> 4
    vals = E2M1[nib] * np.repeat(np.exp2(scales.astype(np.float64) - 127.0), 8, axis=1)[..., None]
    return vals.transpose(0, 1, 3, 2).reshape(g * 512, n)


def planes(y):
    n, m = y.shape
    v = y.astype(np.float32).astype(ml_dtypes.bfloat16).astype(np.float64).reshape(n // 32, 32, m)
    top = np.abs(v).max(1)
    byte = np.clip(np.where(top > 0, np.frexp(top)[1] - 1 + 127 - 7, 1), 1, 254)
    codes = (v * np.exp2(127.0 - byte)[:, None, :]).reshape(n, m).astype(np.float32).astype(ml_dtypes.float8_e4m3fn).view(np.uint8)
    words = codes.reshape(n // 512, 128, 4, m).transpose(0, 1, 3, 2)
    return np.ascontiguousarray(words), np.ascontiguousarray(byte.astype(np.uint8).reshape(n // 512, 16, m))


K, T, S, N, H = 1024, 1024, 512, 512, 512


def setup_inputs():
    n = np.random.standard_normal
    s = mx_kscale(K)[:, None]
    u = mx_kscale(H)
    packed_xT = pack_weight(n((K, T)) * s)
    packed_w1 = pack_fp4(n((K, N)) / np.sqrt(K) / s)
    packed_w2 = pack_fp4(n((H, N)) / np.sqrt(H) / u[:, None])
    return {
        "x_words": packed_xT[0],
        "x_scales": packed_xT[1],
        "w1_words": packed_w1[0],
        "w1_scales": packed_w1[1],
        "unit": (np.random.uniform(0.6, 1.4, (H, 1)) * u[:, None]).astype(np.float32),
        "w2_words": packed_w2[0],
        "w2_scales": packed_w2[1],
        "offs": striped(np.random.permutation(T)[:S]),
        "n1": striped(np.random.permutation(S)),
        "n2": striped(np.random.permutation(S)),
        "n3": striped(np.random.permutation(S)),
    }


def reference(x_words, x_scales, w1_words, w1_scales, unit, w2_words, w2_scales, offs, n1, n2, n3):
    xq = unpack_weight(x_words, x_scales)[:, unstriped(offs)]
    y = unpack_fp4(w1_words, w1_scales).T @ xq
    y1 = y[:, unstriped(n1)]
    y2 = y[:, unstriped(n2)]
    hop1 = y1 + y2
    h12 = hop1[:, unstriped(n2)]
    h13 = hop1[:, unstriped(n3)]
    hop2 = 0.6 * (h12 + h13)
    back = hop2 - (1.2 * y)
    hid = f64(unit) * (hop1 * np.tanh(back))
    out_0 = unpack_fp4(w2_words, w2_scales).T @ mxq(hid, 0, "e4m3")
    return (out_0,) + planes(out_0)

@@ -1,0 +1,233 @@
+from contextlib import ExitStack
+
+import concourse.mybir as mybir
+
+K, T, S, N, H = 1024, 1024, 512, 512, 512
+FLOPS = 2 * K * H * S + 2 * H * N * S
+
+F32 = mybir.dt.float32
+BF16 = mybir.dt.bfloat16
+I32 = mybir.dt.int32
+U32 = mybir.dt.uint32
+U16 = mybir.dt.uint16
+U8 = mybir.dt.uint8
+FP8X4 = mybir.dt.float8_e4m3fn_x4
+FP4X4 = mybir.dt.float4_e2m1fn_x4
+ACT = mybir.ActivationFunctionType
+ALU = mybir.AluOpType
+
+P = 128
+PACK = 4
+PASSES = K // (P * PACK)
+SPARE = 16
+CHUNKS = (128, 128, 128, 128,)
+WHOLE = 3
+EV = "SVSS"
+G1 = "HSSS"
+SEC = "DDEE"
+HW = "SVVV"
+RW = "VVVS"
+RE = "SSSV"
+BANK = 512
+
+
+def tile_picked_ytwohop_mul_po_kernel(
+    tc, x_words, x_scales, w1_words, w1_scales, unit, w2_words, w2_scales, offs, n1, n2, n3, out_0, out_1, out_2
+):
+    nc = tc.nc
+    with ExitStack() as ctx:
+        keep = ctx.enter_context(tc.tile_pool(name="keep", bufs=1))
+        psum = ctx.enter_context(tc.psum_pool(name="psum", bufs=1))
+
+        offs_t = keep.tile([P, S // 16], U16, name="offs_t")
+        n1_t = keep.tile([P, S // 16], U16, name="n1_t")
+        n2_t = keep.tile([P, S // 16], U16, name="n2_t")
+        n3_t = keep.tile([P, S // 16], U16, name="n3_t")
+
+        xs_raw = keep.tile([P, T], U8, name="xs_raw", align_bytes=64)
+        xw_raw = [keep.tile([P, T], I32, name=f"xw_raw{o}", align_bytes=64) for o in range(PASSES)]
+        w1w_raw = keep.tile([P, PASSES, 2 * H], U8, name="w1w_raw", align_bytes=64)
+        w1s_raw = keep.tile([P, PASSES, H], U8, name="w1s_raw", align_bytes=64)
+        unit_t = keep.tile([P, PACK], F32, name="unit_t")
+        xs_both = keep.tile([P, S], U8, name="xs_both", align_bytes=64)
+        xs_second = keep.tile([P, S], U8, name="xs_second", align_bytes=64)
+        y = [keep.tile([P, S + SPARE], F32, name=f"y{t}", align_bytes=64) for t in range(PACK)]
+
+        hop1 = [keep.tile([P, S + SPARE], F32, name=f"hop1_{t}", align_bytes=64) for t in range(PACK)]
+        nc.gpsimd.memset(xs_raw[:].bitcast(I32), 0)
+        nc.gpsimd.memset(w1s_raw[:].rearrange("p o c -> p (o c)").bitcast(I32), 0)
+        nc.gpsimd.memset(xs_second[:].bitcast(I32), 0)
+        for window in y + hop1:
+            nc.gpsimd.memset(window[:, S:], 0.0)
+
+        nc.sync.dma_start(offs_t[:], offs)
+        for q in range(4):
+            nc.sync.dma_start(xs_raw[32 * q : 32 * q + 8, :].bitcast(I32), x_scales[:, 4 * q : 4 * q + 4, :].bitcast(I32))
+        nc.sync.dma_start(xw_raw[0][:], x_words[0].rearrange("p c r -> p (c r)").bitcast(I32))
+        nc.sync.dma_start(xw_raw[1][:], x_words[1].rearrange("p c r -> p (c r)").bitcast(I32))
+        nc.sync.dma_start(w1w_raw[:].bitcast(I32), w1_words.rearrange("o p c -> p o c").bitcast(I32))
+        for q in range(4):
+            nc.sync.dma_start(
+                w1s_raw[32 * q : 32 * q + 4, :, :].bitcast(I32),
+                w1_scales[:, 4 * q : 4 * q + 4, :].rearrange("o r c -> r o c").bitcast(I32),
+            )
+
+        xw = [keep.tile([P, S], U32, name=f"xw{o}", align_bytes=64) for o in range(PASSES)]
+        nc.vector.tensor_copy(xs_both[:], xs_raw[:].indirect(offs_t[:]))
+        for q in range(4):
+            nc.scalar.dma_start(xs_second[32 * q : 32 * q + 4, :].bitcast(I32), xs_both[32 * q + 4 : 32 * q + 8, :].bitcast(I32))
+        for o in range(PASSES):
+            nc.vector.tensor_copy(xw[o][:], xw_raw[o][:].bitcast(U32).indirect(offs_t[:]))
+        xs = [xs_both, xs_second]
+
+        nc.sync.dma_start(n1_t[:], n1)
+        nc.sync.dma_start(n2_t[:], n2)
+        nc.sync.dma_start(n3_t[:], n3)
+        nc.sync.dma_start(unit_t[:], unit.rearrange("(p t) one -> p (t one)", t=PACK))
+
+        w1w = keep.tile([P, PASSES, 2 * H], U8, name="w1w", align_bytes=64)
+        w1s = [keep.tile([P, PASSES, P], U8, name=f"w1s{t}", align_bytes=64) for t in range(PACK)]
+        nc.scalar.copy(
+            w1w[:].bitcast(U16).rearrange("p o (t m) -> p o t m", t=PACK),
+            w1w_raw[:].bitcast(U16).rearrange("p o (m t) -> p o t m", t=PACK),
+        )
+        for t in range(PACK):
+            nc.gpsimd.tensor_copy(w1s[t][:], w1s_raw[:].rearrange("p o (m t) -> p t o m", t=PACK)[:, t])
+        w2w_raw = w1w_raw[:, 0, :]
+        w2s_raw = w1s_raw[:, 0, :]
+        nc.sync.dma_start(w2w_raw.bitcast(I32), w2_words[0].bitcast(I32))
+        for q in range(4):
+            nc.sync.dma_start(w1s_raw[32 * q : 32 * q + 4, 0, :].bitcast(I32), w2_scales[0, 4 * q : 4 * q + 4, :].bitcast(I32))
+        w2w = keep.tile([P, 2 * N], U8, name="w2w", align_bytes=64)
+        w2s = keep.tile([P, N], U8, name="w2s", align_bytes=64)
+        nc.scalar.copy(
+            w2w[:].bitcast(U16).rearrange("p (t m) -> p t m", t=PACK),
+            w2w_raw.bitcast(U16).rearrange("p (m t) -> p t m", t=PACK),
+        )
+        nc.gpsimd.tensor_copy(w2s[:].rearrange("p (t m) -> p t m", t=PACK), w2s_raw.rearrange("p (m t) -> p t m", t=PACK))
+
+        def eng_copy(e, out, in_):
+            if e == "V":
+                nc.vector.tensor_copy(out, in_)
+            else:
+                nc.scalar.copy(out, in_)
+
+        def gather(e, out, window, lst):
+            if e == "V":
+                nc.vector.tensor_copy(out, window.indirect(lst))
+            else:
+                nc.scalar.activation(out, window.indirect(lst), ACT.Copy)
+
+        part = [keep.tile([P, S], F32, name=f"part{t}", align_bytes=64) for t in range(PACK)]
+        arg = [keep.tile([P, S], F32, name=f"arg{t}", align_bytes=64) for t in range(PACK)]
+        gate = [keep.tile([P, S], F32, name=f"gate{t}", align_bytes=64) for t in range(PACK)]
+        hid = keep.tile([P, PACK, S], BF16, name="hid", align_bytes=64)
+
+        def first(t):
+            acc = psum.tile([P, S], F32, name=f"y_acc{t}")
+            for o in range(PASSES):
+                nc.tensor.matmul_mx(
+                    acc[:],
+                    lhsT=w1w[:, o, 2 * P * t : 2 * P * (t + 1)].bitcast(FP4X4),
+                    lhsT_scale=w1s[t][:, o, :],
+                    rhs=xw[o][:].bitcast(FP8X4),
+                    rhs_scale=xs[o][:],
+                    start=(o == 0),
+                    stop=(o == PASSES - 1),
+                )
+            eng_copy(EV[t], y[t][:, :S], acc[:])
+            y1 = keep.tile([P, S], F32, name=f"y1_{t}", align_bytes=64)
+            if G1[t] == "S":
+                gather("S", y1[:], y[t][:], n1_t[:])
+            else:
+                gather("V", y1[:, : S // 2], y[t][:], n1_t[:, : S // 32])
+                gather("S" if G1[t] == "H" else "V", y1[:, S // 2 :], y[t][:], n1_t[:, S // 32 :])
+            nc.vector.tensor_tensor(hop1[t][:, :S], y[t][:].indirect(n2_t[:]), y1[:], ALU.add)
+
+        def mid(t):
+            h12 = keep.tile([P, S], F32, name=f"h12_{t}", align_bytes=64)
+            gather("S", h12[:], hop1[t][:], n2_t[:])
+            nc.vector.scalar_tensor_tensor(part[t][:], y[t][:, :S], -2.0, h12[:], ALU.mult, ALU.add)
+
+        h13 = {t: keep.tile([P, S], F32, name=f"h13_{t}", align_bytes=64) for t in range(PACK) if SEC[t] == "E"}
+
+        def second(t, c0, width):
+            cols = slice(c0, c0 + width)
+            lst = n3_t[:, c0 // 16 : (c0 + width) // 16]
+            if SEC[t] == "D":
+                nc.vector.tensor_tensor(arg[t][:, cols], hop1[t][:].indirect(lst), part[t][:, cols], ALU.add)
+            else:
+                gather("S", h13[t][:, cols], hop1[t][:], lst)
+                nc.vector.tensor_tensor(arg[t][:, cols], h13[t][:, cols], part[t][:, cols], ALU.add)
+
+        def squash(t, c0, width):
+            cols = slice(c0, c0 + width)
+            nc.scalar.activation(gate[t][:, cols], arg[t][:, cols], ACT.Tanh, scale=0.6)
+
+        def hidden(t, c0, width):
+            cols = slice(c0, c0 + width)
+            nc.vector.scalar_tensor_tensor(
+                hid[:, t, cols], hop1[t][:, cols], unit_t[:, t : t + 1], gate[t][:, cols], ALU.mult, ALU.mult
+            )
+
+        first(0)
+        for t in range(PACK):
+            if t + 1 < PACK:
+                first(t + 1)
+            mid(t)
+            if t < WHOLE:
+                second(t, 0, S)
+                squash(t, 0, S)
+                hidden(t, 0, S)
+
+        out_words = keep.tile([P, S], U32, name="out_words", align_bytes=64)
+        out_scales = keep.tile([P, S], U8, name="out_scales", align_bytes=64)
+        out_rows = out_0.rearrange("(p t) j -> p t j", t=PACK)
+        out_words_dram = out_1[0].rearrange("p c r -> p (c r)").bitcast(I32)
+        c0 = 0
+        for c, width in enumerate(CHUNKS):
+            cols = slice(c0, c0 + width)
+            for step in (second, squash, hidden):
+                for t in range(WHOLE, PACK):
+                    step(t, c0, width)
+            c0 = c0 + width
+            hid_woven = keep.tile([P, width, PACK], BF16, name=f"hid_woven{c}", align_bytes=64)
+            hid_words = keep.tile([P, width], U32, name=f"hid_words{c}", align_bytes=64)
+            hid_scales = keep.tile([P, width], U8, name=f"hid_scales{c}", align_bytes=64)
+            eng_copy(
+                HW[c],
+                hid_woven[:].rearrange("p (c i) t -> p c t i", i=4),
+                hid[:, :, cols].rearrange("p t (c i) -> p c t i", i=4),
+            )
+            nc.vector.quantize_mx(hid_words[:].bitcast(FP8X4), hid_scales[:], hid_woven[:].rearrange("p c t -> p (c t)"))
+            res = keep.tile([P, PACK, width], F32, name=f"res{c}", align_bytes=64)
+            res_woven = keep.tile([P, width, PACK], BF16, name=f"res_woven{c}", align_bytes=64)
+            per_bank = BANK // width
+            for b in range(PACK // per_bank):
+                acc2 = psum.tile([P, per_bank, width], F32, name=f"out_acc{c}_{b}")
+                for u in range(per_bank):
+                    t = b * per_bank + u
+                    nc.tensor.matmul_mx(
+                        acc2[:, u, :],
+                        lhsT=w2w[:, 2 * P * t : 2 * P * (t + 1)].bitcast(FP4X4),
+                        lhsT_scale=w2s[:, P * t : P * (t + 1)],
+                        rhs=hid_words[:].bitcast(FP8X4),
+                        rhs_scale=hid_scales[:],
+                        start=True,
+                        stop=True,
+                    )
+                if RW[c] == "S":
+                    nc.scalar.copy(res_woven[:], acc2[:].rearrange("p t c -> p c t"))
+                eng_copy(RE[c], res[:, b * per_bank : (b + 1) * per_bank, :], acc2[:])
+            nc.sync.dma_start(out_rows[:, :, cols], res[:])
+            if RW[c] == "V":
+                nc.vector.tensor_copy(
+                    res_woven[:].rearrange("p (c i) t -> p c t i", i=4), res[:].rearrange("p t (c i) -> p c t i", i=4)
+                )
+            nc.vector.quantize_mx(
+                out_words[:, cols].bitcast(FP8X4), out_scales[:, cols], res_woven[:].rearrange("p c t -> p (c t)")
+            )
+            nc.sync.dma_start(out_words_dram[:, cols], out_words[:, cols].bitcast(I32))
+        for q in range(4):
+            queue = nc.sync if q % 2 == 0 else nc.scalar
+            queue.dma_start(out_2[0, 4 * q : 4 * q + 4, :].bitcast(I32), out_scales[32 * q : 32 * q + 4, :].bitcast(I32))

@@ -18,17 +18,17 @@ ALU = mybir.AluOpType
 
 P = 128
 PACK = 4
+QUADS = 4
 PASSES = K // (P * PACK)
-SPARE = 16
-CHUNKS = (128, 128, 128, 128,)
-WHOLE = 3
-EV = "SVSS"
-G1 = "HSSS"
-SEC = "DDEE"
-HW = "SVVV"
-RW = "VVVS"
-RE = "SSSV"
-BANK = 512
+GROUP = 16
+HALF = S // 2
+Y_SPARE = 192
+HOP_SPARE = 16
+CHUNK = 128
+CHUNKS = S // CHUNK
+EARLY = 2
+LATE = PACK - EARLY
+SCALAR_WEAVES = 2
 
 
 def tile_picked_ytwohop_mul_po_kernel(
@@ -37,197 +37,188 @@ def tile_picked_ytwohop_mul_po_kernel(
     nc = tc.nc
     with ExitStack() as ctx:
         keep = ctx.enter_context(tc.tile_pool(name="keep", bufs=1))
-        psum = ctx.enter_context(tc.psum_pool(name="psum", bufs=1))
+        psum = ctx.enter_context(tc.psum_pool(name="psum", bufs=8))
 
-        offs_t = keep.tile([P, S // 16], U16, name="offs_t")
-        n1_t = keep.tile([P, S // 16], U16, name="n1_t")
-        n2_t = keep.tile([P, S // 16], U16, name="n2_t")
-        n3_t = keep.tile([P, S // 16], U16, name="n3_t")
+        def sb(shape, dtype, name):
+            return keep.tile(shape, dtype, name=name, align_bytes=64)
 
-        xs_raw = keep.tile([P, T], U8, name="xs_raw", align_bytes=64)
-        xw_raw = [keep.tile([P, T], I32, name=f"xw_raw{o}", align_bytes=64) for o in range(PASSES)]
-        w1w_raw = keep.tile([P, PASSES, 2 * H], U8, name="w1w_raw", align_bytes=64)
-        w1s_raw = keep.tile([P, PASSES, H], U8, name="w1s_raw", align_bytes=64)
-        unit_t = keep.tile([P, PACK], F32, name="unit_t")
-        xs_both = keep.tile([P, S], U8, name="xs_both", align_bytes=64)
-        xs_second = keep.tile([P, S], U8, name="xs_second", align_bytes=64)
-        y = [keep.tile([P, S + SPARE], F32, name=f"y{t}", align_bytes=64) for t in range(PACK)]
+        def entries(lst, start, count):
+            return lst[:, start // GROUP : (start + count) // GROUP]
 
-        hop1 = [keep.tile([P, S + SPARE], F32, name=f"hop1_{t}", align_bytes=64) for t in range(PACK)]
-        nc.gpsimd.memset(xs_raw[:].bitcast(I32), 0)
-        nc.gpsimd.memset(w1s_raw[:].rearrange("p o c -> p (o c)").bitcast(I32), 0)
-        nc.gpsimd.memset(xs_second[:].bitcast(I32), 0)
+        offs_t, n1_t, n2_t, n3_t = [sb([P, S // GROUP], U16, name) for name in ("offs_t", "n1_t", "n2_t", "n3_t")]
+        xs_raw = sb([P, PASSES, T], U8, "xs_raw")
+        xw_raw = [sb([P, T], I32, f"xw_raw{o}") for o in range(PASSES)]
+        w1w_raw = sb([P, PASSES, 2 * H], U8, "w1w_raw")
+        w1s_raw = sb([P, PASSES, H], U8, "w1s_raw")
+        w2w_raw = sb([P, 2 * N], U8, "w2w_raw")
+        w2s_raw = sb([P, 1, N], U8, "w2s_raw")
+        unit_t = sb([P, PACK], F32, "unit_t")
+        y = [sb([P, S + Y_SPARE], F32, f"y{t}") for t in range(PACK)]
+        hop1 = [sb([P, S + HOP_SPARE], F32, f"hop1_{t}") for t in range(PACK)]
+
+        nc.gpsimd.memset(xs_raw[:].rearrange("p o c -> p (o c)").bitcast(I32), 0)
+        nc.vector.memset(w1s_raw[:].rearrange("p o c -> p (o c)").bitcast(I32), 0)
+        nc.vector.memset(w2s_raw[:, 0, :].bitcast(I32), 0)
         for window in y + hop1:
-            nc.gpsimd.memset(window[:, S:], 0.0)
+            nc.vector.memset(window[:, S:], 0.0)
+
+        def load_scales(dst, src):
+            for q in range(QUADS):
+                nc.sync.dma_start(
+                    dst[32 * q : 32 * q + 4, :, :].bitcast(I32),
+                    src[:, 4 * q : 4 * q + 4, :].rearrange("o r c -> r o c").bitcast(I32),
+                )
+
+        def load_x_words(o):
+            nc.sync.dma_start(xw_raw[o][:], x_words[o].rearrange("p c r -> p (c r)").bitcast(I32))
 
         nc.sync.dma_start(offs_t[:], offs)
-        for q in range(4):
-            nc.sync.dma_start(xs_raw[32 * q : 32 * q + 8, :].bitcast(I32), x_scales[:, 4 * q : 4 * q + 4, :].bitcast(I32))
-        nc.sync.dma_start(xw_raw[0][:], x_words[0].rearrange("p c r -> p (c r)").bitcast(I32))
-        nc.sync.dma_start(xw_raw[1][:], x_words[1].rearrange("p c r -> p (c r)").bitcast(I32))
-        nc.sync.dma_start(w1w_raw[:].bitcast(I32), w1_words.rearrange("o p c -> p o c").bitcast(I32))
-        for q in range(4):
-            nc.sync.dma_start(
-                w1s_raw[32 * q : 32 * q + 4, :, :].bitcast(I32),
-                w1_scales[:, 4 * q : 4 * q + 4, :].rearrange("o r c -> r o c").bitcast(I32),
-            )
-
-        xw = [keep.tile([P, S], U32, name=f"xw{o}", align_bytes=64) for o in range(PASSES)]
-        nc.vector.tensor_copy(xs_both[:], xs_raw[:].indirect(offs_t[:]))
-        for q in range(4):
-            nc.scalar.dma_start(xs_second[32 * q : 32 * q + 4, :].bitcast(I32), xs_both[32 * q + 4 : 32 * q + 8, :].bitcast(I32))
-        for o in range(PASSES):
-            nc.vector.tensor_copy(xw[o][:], xw_raw[o][:].bitcast(U32).indirect(offs_t[:]))
-        xs = [xs_both, xs_second]
-
+        load_scales(xs_raw, x_scales)
         nc.sync.dma_start(n1_t[:], n1)
         nc.sync.dma_start(n2_t[:], n2)
+        load_x_words(0)
+        nc.sync.dma_start(w1w_raw[:].bitcast(I32), w1_words.rearrange("o p c -> p o c").bitcast(I32))
+        load_scales(w1s_raw, w1_scales)
+        load_x_words(1)
         nc.sync.dma_start(n3_t[:], n3)
+        load_scales(w2s_raw, w2_scales)
+        nc.sync.dma_start(w2w_raw[:].bitcast(I32), w2_words[0].bitcast(I32))
         nc.sync.dma_start(unit_t[:], unit.rearrange("(p t) one -> p (t one)", t=PACK))
 
-        w1w = keep.tile([P, PASSES, 2 * H], U8, name="w1w", align_bytes=64)
-        w1s = [keep.tile([P, PASSES, P], U8, name=f"w1s{t}", align_bytes=64) for t in range(PACK)]
+        xs = [sb([P, S], U8, f"xs{o}") for o in range(PASSES)]
+        xw = [sb([P, S], U32, f"xw{o}") for o in range(PASSES)]
+        for o in range(PASSES):
+            nc.vector.tensor_copy(xs[o][:], xs_raw[:, o, :].indirect(offs_t[:]))
+        nc.vector.tensor_copy(xw[0][:], xw_raw[0][:].bitcast(U32).indirect(offs_t[:]))
+        for h0 in (0, HALF):
+            nc.vector.tensor_copy(
+                xw[1][:, h0 : h0 + HALF], xw_raw[1][:].bitcast(U32).indirect(entries(offs_t, h0, HALF))
+            )
+
+        w1w = sb([P, PASSES, 2 * H], U8, "w1w")
+        w1s = [sb([P, PASSES, P], U8, f"w1s{t}") for t in range(PACK)]
+        w2w = sb([P, 2 * N], U8, "w2w")
+        w2s = sb([P, N], U8, "w2s")
         nc.scalar.copy(
             w1w[:].bitcast(U16).rearrange("p o (t m) -> p o t m", t=PACK),
             w1w_raw[:].bitcast(U16).rearrange("p o (m t) -> p o t m", t=PACK),
         )
         for t in range(PACK):
             nc.gpsimd.tensor_copy(w1s[t][:], w1s_raw[:].rearrange("p o (m t) -> p t o m", t=PACK)[:, t])
-        w2w_raw = w1w_raw[:, 0, :]
-        w2s_raw = w1s_raw[:, 0, :]
-        nc.sync.dma_start(w2w_raw.bitcast(I32), w2_words[0].bitcast(I32))
-        for q in range(4):
-            nc.sync.dma_start(w1s_raw[32 * q : 32 * q + 4, 0, :].bitcast(I32), w2_scales[0, 4 * q : 4 * q + 4, :].bitcast(I32))
-        w2w = keep.tile([P, 2 * N], U8, name="w2w", align_bytes=64)
-        w2s = keep.tile([P, N], U8, name="w2s", align_bytes=64)
         nc.scalar.copy(
             w2w[:].bitcast(U16).rearrange("p (t m) -> p t m", t=PACK),
-            w2w_raw.bitcast(U16).rearrange("p (m t) -> p t m", t=PACK),
+            w2w_raw[:].bitcast(U16).rearrange("p (m t) -> p t m", t=PACK),
         )
-        nc.gpsimd.tensor_copy(w2s[:].rearrange("p (t m) -> p t m", t=PACK), w2s_raw.rearrange("p (m t) -> p t m", t=PACK))
+        nc.gpsimd.tensor_copy(w2s[:].rearrange("p (t m) -> p t m", t=PACK), w2s_raw[:, 0, :].rearrange("p (m t) -> p t m", t=PACK))
 
-        def eng_copy(e, out, in_):
-            if e == "V":
-                nc.vector.tensor_copy(out, in_)
-            else:
-                nc.scalar.copy(out, in_)
-
-        def gather(e, out, window, lst):
-            if e == "V":
-                nc.vector.tensor_copy(out, window.indirect(lst))
-            else:
-                nc.scalar.activation(out, window.indirect(lst), ACT.Copy)
-
-        part = [keep.tile([P, S], F32, name=f"part{t}", align_bytes=64) for t in range(PACK)]
-        arg = [keep.tile([P, S], F32, name=f"arg{t}", align_bytes=64) for t in range(PACK)]
-        gate = [keep.tile([P, S], F32, name=f"gate{t}", align_bytes=64) for t in range(PACK)]
-        hid = keep.tile([P, PACK, S], BF16, name="hid", align_bytes=64)
-
-        def first(t):
-            acc = psum.tile([P, S], F32, name=f"y_acc{t}")
+        def first_product(t, c0, width):
+            cols = slice(c0, c0 + width)
+            acc = psum.tile([P, width], F32, name=f"y_acc{t}_{c0}", tag="bank")
             for o in range(PASSES):
                 nc.tensor.matmul_mx(
                     acc[:],
                     lhsT=w1w[:, o, 2 * P * t : 2 * P * (t + 1)].bitcast(FP4X4),
                     lhsT_scale=w1s[t][:, o, :],
-                    rhs=xw[o][:].bitcast(FP8X4),
-                    rhs_scale=xs[o][:],
+                    rhs=xw[o][:, cols].bitcast(FP8X4),
+                    rhs_scale=xs[o][:, cols],
                     start=(o == 0),
                     stop=(o == PASSES - 1),
                 )
-            eng_copy(EV[t], y[t][:, :S], acc[:])
-            y1 = keep.tile([P, S], F32, name=f"y1_{t}", align_bytes=64)
-            if G1[t] == "S":
-                gather("S", y1[:], y[t][:], n1_t[:])
+            return acc
+
+        for t in range(PACK):
+            y1 = sb([P, S], F32, f"y1_{t}")
+            if t == 0:
+                nc.scalar.copy(y[t][:, :HALF], first_product(t, 0, HALF)[:])
+                nc.vector.tensor_copy(y[t][:, HALF:S], first_product(t, HALF, HALF)[:])
+                nc.vector.tensor_copy(y1[:, :HALF], y[t][:].indirect(entries(n1_t, 0, HALF)))
+                nc.scalar.activation(y1[:, HALF:], y[t][:].indirect(entries(n1_t, HALF, HALF)), ACT.Copy)
             else:
-                gather("V", y1[:, : S // 2], y[t][:], n1_t[:, : S // 32])
-                gather("S" if G1[t] == "H" else "V", y1[:, S // 2 :], y[t][:], n1_t[:, S // 32 :])
+                nc.scalar.copy(y[t][:, :S], first_product(t, 0, S)[:])
+                if t < EARLY:
+                    nc.vector.tensor_copy(y1[:], y[t][:].indirect(n1_t[:]))
+                else:
+                    nc.scalar.activation(y1[:], y[t][:].indirect(n1_t[:]), ACT.Copy)
             nc.vector.tensor_tensor(hop1[t][:, :S], y[t][:].indirect(n2_t[:]), y1[:], ALU.add)
 
-        def mid(t):
-            h12 = keep.tile([P, S], F32, name=f"h12_{t}", align_bytes=64)
-            gather("S", h12[:], hop1[t][:], n2_t[:])
-            nc.vector.scalar_tensor_tensor(part[t][:], y[t][:, :S], -2.0, h12[:], ALU.mult, ALU.add)
+        hid = sb([P, PACK, S], BF16, "hid")
 
-        h13 = {t: keep.tile([P, S], F32, name=f"h13_{t}", align_bytes=64) for t in range(PACK) if SEC[t] == "E"}
-
-        def second(t, c0, width):
-            cols = slice(c0, c0 + width)
-            lst = n3_t[:, c0 // 16 : (c0 + width) // 16]
-            if SEC[t] == "D":
-                nc.vector.tensor_tensor(arg[t][:, cols], hop1[t][:].indirect(lst), part[t][:, cols], ALU.add)
-            else:
-                gather("S", h13[t][:, cols], hop1[t][:], lst)
-                nc.vector.tensor_tensor(arg[t][:, cols], h13[t][:, cols], part[t][:, cols], ALU.add)
-
-        def squash(t, c0, width):
-            cols = slice(c0, c0 + width)
-            nc.scalar.activation(gate[t][:, cols], arg[t][:, cols], ACT.Tanh, scale=0.6)
-
-        def hidden(t, c0, width):
-            cols = slice(c0, c0 + width)
+        def hidden(t, cols, gate_cols):
             nc.vector.scalar_tensor_tensor(
-                hid[:, t, cols], hop1[t][:, cols], unit_t[:, t : t + 1], gate[t][:, cols], ALU.mult, ALU.mult
+                hid[:, t, cols], hop1[t][:, cols], unit_t[:, t : t + 1], gate_cols, ALU.mult, ALU.mult
             )
 
-        first(0)
+        part_late = sb([P, LATE, S], F32, "part_late")
         for t in range(PACK):
-            if t + 1 < PACK:
-                first(t + 1)
-            mid(t)
-            if t < WHOLE:
-                second(t, 0, S)
-                squash(t, 0, S)
-                hidden(t, 0, S)
+            h12 = sb([P, S], F32, f"h12_{t}")
+            part = sb([P, S], F32, f"part{t}")[:] if t < EARLY else part_late[:, t - EARLY, :]
+            nc.scalar.activation(h12[:], hop1[t][:].indirect(n2_t[:]), ACT.Copy)
+            nc.vector.scalar_tensor_tensor(part, y[t][:, :S], -2.0, h12[:], ALU.mult, ALU.add)
+            if t < EARLY:
+                arg = sb([P, S], F32, f"arg{t}")
+                gate = sb([P, S], F32, f"gate{t}")
+                nc.vector.tensor_tensor(arg[:], hop1[t][:].indirect(n3_t[:]), part, ALU.add)
+                nc.scalar.activation(gate[:], arg[:], ACT.Tanh, scale=0.6)
+                hidden(t, slice(0, S), gate[:])
 
-        out_words = keep.tile([P, S], U32, name="out_words", align_bytes=64)
-        out_scales = keep.tile([P, S], U8, name="out_scales", align_bytes=64)
+        out_words = sb([P, S], U32, "out_words")
+        out_scales = sb([P, S], U8, "out_scales")
         out_rows = out_0.rearrange("(p t) j -> p t j", t=PACK)
         out_words_dram = out_1[0].rearrange("p c r -> p (c r)").bitcast(I32)
-        c0 = 0
-        for c, width in enumerate(CHUNKS):
-            cols = slice(c0, c0 + width)
-            for step in (second, squash, hidden):
-                for t in range(WHOLE, PACK):
-                    step(t, c0, width)
-            c0 = c0 + width
-            hid_woven = keep.tile([P, width, PACK], BF16, name=f"hid_woven{c}", align_bytes=64)
-            hid_words = keep.tile([P, width], U32, name=f"hid_words{c}", align_bytes=64)
-            hid_scales = keep.tile([P, width], U8, name=f"hid_scales{c}", align_bytes=64)
-            eng_copy(
-                HW[c],
-                hid_woven[:].rearrange("p (c i) t -> p c t i", i=4),
-                hid[:, :, cols].rearrange("p t (c i) -> p c t i", i=4),
-            )
-            nc.vector.quantize_mx(hid_words[:].bitcast(FP8X4), hid_scales[:], hid_woven[:].rearrange("p c t -> p (c t)"))
-            res = keep.tile([P, PACK, width], F32, name=f"res{c}", align_bytes=64)
-            res_woven = keep.tile([P, width, PACK], BF16, name=f"res_woven{c}", align_bytes=64)
-            per_bank = BANK // width
-            for b in range(PACK // per_bank):
-                acc2 = psum.tile([P, per_bank, width], F32, name=f"out_acc{c}_{b}")
-                for u in range(per_bank):
-                    t = b * per_bank + u
-                    nc.tensor.matmul_mx(
-                        acc2[:, u, :],
-                        lhsT=w2w[:, 2 * P * t : 2 * P * (t + 1)].bitcast(FP4X4),
-                        lhsT_scale=w2s[:, P * t : P * (t + 1)],
-                        rhs=hid_words[:].bitcast(FP8X4),
-                        rhs_scale=hid_scales[:],
-                        start=True,
-                        stop=True,
-                    )
-                if RW[c] == "S":
-                    nc.scalar.copy(res_woven[:], acc2[:].rearrange("p t c -> p c t"))
-                eng_copy(RE[c], res[:, b * per_bank : (b + 1) * per_bank, :], acc2[:])
-            nc.sync.dma_start(out_rows[:, :, cols], res[:])
-            if RW[c] == "V":
-                nc.vector.tensor_copy(
-                    res_woven[:].rearrange("p (c i) t -> p c t i", i=4), res[:].rearrange("p t (c i) -> p c t i", i=4)
+
+        def woven(tile):
+            return tile.rearrange("p (c i) t -> p c t i", i=4)
+
+        def planes(tile):
+            return tile.rearrange("p t (c i) -> p c t i", i=4)
+
+        for c in range(CHUNKS):
+            cols = slice(c * CHUNK, (c + 1) * CHUNK)
+            h13 = sb([P, LATE, CHUNK], F32, f"h13_{c}")
+            arg = sb([P, LATE, CHUNK], F32, f"arg_late{c}")
+            gate = sb([P, LATE, CHUNK], F32, f"gate_late{c}")
+            for u in range(LATE):
+                nc.scalar.activation(
+                    h13[:, u, :], hop1[EARLY + u][:].indirect(entries(n3_t, c * CHUNK, CHUNK)), ACT.Copy
                 )
+            nc.vector.tensor_tensor(arg[:], h13[:], part_late[:, :, cols], ALU.add)
+            nc.scalar.activation(gate[:], arg[:], ACT.Tanh, scale=0.6)
+            for u in range(LATE):
+                hidden(EARLY + u, cols, gate[:, u, :])
+
+            hid_woven = sb([P, CHUNK, PACK], BF16, f"hid_woven{c}")
+            hid_words = sb([P, CHUNK], U32, f"hid_words{c}")
+            hid_scales = sb([P, CHUNK], U8, f"hid_scales{c}")
+            if c < SCALAR_WEAVES:
+                nc.scalar.copy(woven(hid_woven[:]), planes(hid[:, :, cols]))
+            else:
+                nc.vector.tensor_copy(woven(hid_woven[:]), planes(hid[:, :, cols]))
+            nc.vector.quantize_mx(hid_words[:].bitcast(FP8X4), hid_scales[:], hid_woven[:].rearrange("p c t -> p (c t)"))
+
+            acc = psum.tile([P, PACK, CHUNK], F32, name=f"out_acc{c}", tag="bank")
+            for t in range(PACK):
+                nc.tensor.matmul_mx(
+                    acc[:, t, :],
+                    lhsT=w2w[:, 2 * P * t : 2 * P * (t + 1)].bitcast(FP4X4),
+                    lhsT_scale=w2s[:, P * t : P * (t + 1)],
+                    rhs=hid_words[:].bitcast(FP8X4),
+                    rhs_scale=hid_scales[:],
+                    start=True,
+                    stop=True,
+                )
+            res = sb([P, PACK, CHUNK], F32, f"res{c}")
+            res_woven = sb([P, CHUNK, PACK], BF16, f"res_woven{c}")
+            if c < CHUNKS - 1:
+                nc.scalar.copy(res[:], acc[:])
+                nc.vector.tensor_copy(woven(res_woven[:]), planes(res[:]))
+            else:
+                nc.scalar.copy(res_woven[:], acc[:].rearrange("p t c -> p c t"))
+                nc.vector.tensor_copy(res[:], acc[:])
+            nc.sync.dma_start(out_rows[:, :, cols], res[:])
             nc.vector.quantize_mx(
                 out_words[:, cols].bitcast(FP8X4), out_scales[:, cols], res_woven[:].rearrange("p c t -> p (c t)")
             )
             nc.sync.dma_start(out_words_dram[:, cols], out_words[:, cols].bitcast(I32))
-        for q in range(4):
+        for q in range(QUADS):
             queue = nc.sync if q % 2 == 0 else nc.scalar
             queue.dma_start(out_2[0, 4 * q : 4 * q + 4, :].bitcast(I32), out_scales[32 * q : 32 * q + 4, :].bitcast(I32))

@@ -26,9 +26,8 @@ Y_SPARE = 192
 HOP_SPARE = 16
 CHUNK = 128
 CHUNKS = S // CHUNK
-EARLY = 2
-LATE = PACK - EARLY
-SCALAR_WEAVES = 2
+SCALAR_SECOND = 2
+VECTOR_WEAVES = 2
 
 
 def tile_picked_ytwohop_mul_po_kernel(
@@ -50,13 +49,13 @@ def tile_picked_ytwohop_mul_po_kernel(
         xw_raw = [sb([P, T], I32, f"xw_raw{o}") for o in range(PASSES)]
         w1w_raw = sb([P, PASSES, 2 * H], U8, "w1w_raw")
         w1s_raw = sb([P, PASSES, H], U8, "w1s_raw")
-        w2w_raw = sb([P, 2 * N], U8, "w2w_raw")
         w2s_raw = sb([P, 1, N], U8, "w2s_raw")
         unit_t = sb([P, PACK], F32, "unit_t")
         y = [sb([P, S + Y_SPARE], F32, f"y{t}") for t in range(PACK)]
         hop1 = [sb([P, S + HOP_SPARE], F32, f"hop1_{t}") for t in range(PACK)]
 
-        nc.gpsimd.memset(xs_raw[:].rearrange("p o c -> p (o c)").bitcast(I32), 0)
+        nc.gpsimd.memset(xs_raw[:, 0, :].bitcast(I32), 0)
+        nc.vector.memset(xs_raw[:, 1, :].bitcast(I32), 0)
         nc.vector.memset(w1s_raw[:].rearrange("p o c -> p (o c)").bitcast(I32), 0)
         nc.vector.memset(w2s_raw[:, 0, :].bitcast(I32), 0)
         for window in y + hop1:
@@ -69,97 +68,98 @@ def tile_picked_ytwohop_mul_po_kernel(
                     src[:, 4 * q : 4 * q + 4, :].rearrange("o r c -> r o c").bitcast(I32),
                 )
 
-        def load_x_words(o):
-            nc.sync.dma_start(xw_raw[o][:], x_words[o].rearrange("p c r -> p (c r)").bitcast(I32))
+        def load_x_words(queue, o):
+            queue.dma_start(xw_raw[o][:], x_words[o].rearrange("p c r -> p (c r)").bitcast(I32))
 
         nc.sync.dma_start(offs_t[:], offs)
+        load_x_words(nc.scalar, 0)
+        nc.scalar.dma_start(w1w_raw[:].bitcast(I32), w1_words.rearrange("o p c -> p o c").bitcast(I32))
         load_scales(xs_raw, x_scales)
         nc.sync.dma_start(n1_t[:], n1)
-        nc.sync.dma_start(n2_t[:], n2)
-        load_x_words(0)
-        nc.sync.dma_start(w1w_raw[:].bitcast(I32), w1_words.rearrange("o p c -> p o c").bitcast(I32))
         load_scales(w1s_raw, w1_scales)
-        load_x_words(1)
+        load_x_words(nc.sync, 1)
+        nc.sync.dma_start(n2_t[:], n2)
         nc.sync.dma_start(n3_t[:], n3)
         load_scales(w2s_raw, w2_scales)
-        nc.sync.dma_start(w2w_raw[:].bitcast(I32), w2_words[0].bitcast(I32))
-        nc.sync.dma_start(unit_t[:], unit.rearrange("(p t) one -> p (t one)", t=PACK))
+        nc.gpsimd.dma_start(unit_t[:], unit.rearrange("(p t) one -> p (t one)", t=PACK))
 
+        halves = [slice(0, HALF), slice(HALF, S)]
         xs = [sb([P, S], U8, f"xs{o}") for o in range(PASSES)]
         xw = [sb([P, S], U32, f"xw{o}") for o in range(PASSES)]
+        nc.vector.tensor_copy(xw[0][:], xw_raw[0][:].bitcast(U32).indirect(offs_t[:]))
         for o in range(PASSES):
             nc.vector.tensor_copy(xs[o][:], xs_raw[:, o, :].indirect(offs_t[:]))
-        nc.vector.tensor_copy(xw[0][:], xw_raw[0][:].bitcast(U32).indirect(offs_t[:]))
-        for h0 in (0, HALF):
-            nc.vector.tensor_copy(
-                xw[1][:, h0 : h0 + HALF], xw_raw[1][:].bitcast(U32).indirect(entries(offs_t, h0, HALF))
-            )
+        for cols in halves:
+            nc.vector.tensor_copy(xw[1][:, cols], xw_raw[1][:].bitcast(U32).indirect(entries(offs_t, cols.start, HALF)))
 
-        w1w = sb([P, PASSES, 2 * H], U8, "w1w")
-        w1s = [sb([P, PASSES, P], U8, f"w1s{t}") for t in range(PACK)]
+        w1w = [sb([P, 2 * H], U8, f"w1w{o}") for o in range(PASSES)]
+        w1s = [[sb([P, P], U8, f"w1s{o}_{t}") for t in range(PACK)] for o in range(PASSES)]
         w2w = sb([P, 2 * N], U8, "w2w")
         w2s = sb([P, N], U8, "w2s")
-        nc.scalar.copy(
-            w1w[:].bitcast(U16).rearrange("p o (t m) -> p o t m", t=PACK),
-            w1w_raw[:].bitcast(U16).rearrange("p o (m t) -> p o t m", t=PACK),
-        )
-        for t in range(PACK):
-            nc.gpsimd.tensor_copy(w1s[t][:], w1s_raw[:].rearrange("p o (m t) -> p t o m", t=PACK)[:, t])
+        for o in range(PASSES):
+            nc.scalar.copy(
+                w1w[o][:].bitcast(U16).rearrange("p (t m) -> p t m", t=PACK),
+                w1w_raw[:, o, :].bitcast(U16).rearrange("p (m t) -> p t m", t=PACK),
+            )
+            for t in range(PACK):
+                nc.gpsimd.tensor_copy(w1s[o][t][:], w1s_raw[:, o, :].rearrange("p (m t) -> p t m", t=PACK)[:, t])
+        w2w_raw = w1w_raw[:, 0, :]
+        nc.sync.dma_start(w2w_raw.bitcast(I32), w2_words[0].bitcast(I32))
         nc.scalar.copy(
             w2w[:].bitcast(U16).rearrange("p (t m) -> p t m", t=PACK),
-            w2w_raw[:].bitcast(U16).rearrange("p (m t) -> p t m", t=PACK),
+            w2w_raw.bitcast(U16).rearrange("p (m t) -> p t m", t=PACK),
         )
         nc.gpsimd.tensor_copy(w2s[:].rearrange("p (t m) -> p t m", t=PACK), w2s_raw[:, 0, :].rearrange("p (m t) -> p t m", t=PACK))
 
-        def first_product(t, c0, width):
-            cols = slice(c0, c0 + width)
-            acc = psum.tile([P, width], F32, name=f"y_acc{t}_{c0}", tag="bank")
+        y_acc = [[psum.tile([P, HALF], F32, name=f"y_acc{t}_{h}", tag="bank") for h in range(2)] for t in range(PACK)]
+        for t in range(PACK):
             for o in range(PASSES):
-                nc.tensor.matmul_mx(
-                    acc[:],
-                    lhsT=w1w[:, o, 2 * P * t : 2 * P * (t + 1)].bitcast(FP4X4),
-                    lhsT_scale=w1s[t][:, o, :],
-                    rhs=xw[o][:, cols].bitcast(FP8X4),
-                    rhs_scale=xs[o][:, cols],
-                    start=(o == 0),
-                    stop=(o == PASSES - 1),
-                )
-            return acc
+                for h, cols in enumerate(halves):
+                    nc.tensor.matmul_mx(
+                        y_acc[t][h][:],
+                        lhsT=w1w[o][:, 2 * P * t : 2 * P * (t + 1)].bitcast(FP4X4),
+                        lhsT_scale=w1s[o][t][:],
+                        rhs=xw[o][:, cols].bitcast(FP8X4),
+                        rhs_scale=xs[o][:, cols],
+                        start=(o == 0),
+                        stop=(o == PASSES - 1),
+                    )
+        for t in range(PACK):
+            for h, cols in enumerate(halves):
+                if t == 0 and h == 1:
+                    nc.vector.tensor_copy(y[t][:, cols], y_acc[t][h][:])
+                else:
+                    nc.scalar.copy(y[t][:, cols], y_acc[t][h][:])
 
+        minus_2y = {}
         for t in range(PACK):
             y1 = sb([P, S], F32, f"y1_{t}")
             if t == 0:
-                nc.scalar.copy(y[t][:, :HALF], first_product(t, 0, HALF)[:])
-                nc.vector.tensor_copy(y[t][:, HALF:S], first_product(t, HALF, HALF)[:])
                 nc.vector.tensor_copy(y1[:, :HALF], y[t][:].indirect(entries(n1_t, 0, HALF)))
                 nc.scalar.activation(y1[:, HALF:], y[t][:].indirect(entries(n1_t, HALF, HALF)), ACT.Copy)
             else:
-                nc.scalar.copy(y[t][:, :S], first_product(t, 0, S)[:])
-                if t < EARLY:
-                    nc.vector.tensor_copy(y1[:], y[t][:].indirect(n1_t[:]))
-                else:
-                    nc.scalar.activation(y1[:], y[t][:].indirect(n1_t[:]), ACT.Copy)
+                nc.scalar.activation(y1[:], y[t][:].indirect(n1_t[:]), ACT.Copy)
             nc.vector.tensor_tensor(hop1[t][:, :S], y[t][:].indirect(n2_t[:]), y1[:], ALU.add)
+            if t >= SCALAR_SECOND:
+                minus_2y[t] = sb([P, S], F32, f"minus_2y{t}")
+                nc.vector.tensor_scalar(minus_2y[t][:], y[t][:, :S], -2.0, None, ALU.mult)
 
-        hid = sb([P, PACK, S], BF16, "hid")
-
-        def hidden(t, cols, gate_cols):
-            nc.vector.scalar_tensor_tensor(
-                hid[:, t, cols], hop1[t][:, cols], unit_t[:, t : t + 1], gate_cols, ALU.mult, ALU.mult
-            )
-
-        part_late = sb([P, LATE, S], F32, "part_late")
+        part = sb([P, PACK, S], F32, "part")
+        scaled = sb([P, PACK, S], F32, "scaled")
+        h13 = sb([P, PACK, HALF], F32, "h13")
+        arg_left = sb([P, PACK, HALF], F32, "arg_left")
         for t in range(PACK):
-            h12 = sb([P, S], F32, f"h12_{t}")
-            part = sb([P, S], F32, f"part{t}")[:] if t < EARLY else part_late[:, t - EARLY, :]
-            nc.scalar.activation(h12[:], hop1[t][:].indirect(n2_t[:]), ACT.Copy)
-            nc.vector.scalar_tensor_tensor(part, y[t][:, :S], -2.0, h12[:], ALU.mult, ALU.add)
-            if t < EARLY:
-                arg = sb([P, S], F32, f"arg{t}")
-                gate = sb([P, S], F32, f"gate{t}")
-                nc.vector.tensor_tensor(arg[:], hop1[t][:].indirect(n3_t[:]), part, ALU.add)
-                nc.scalar.activation(gate[:], arg[:], ACT.Tanh, scale=0.6)
-                hidden(t, slice(0, S), gate[:])
+            if t < SCALAR_SECOND:
+                h12 = sb([P, S], F32, f"h12_{t}")
+                nc.scalar.activation(h12[:], hop1[t][:].indirect(n2_t[:]), ACT.Copy)
+                nc.vector.scalar_tensor_tensor(part[:, t, :], y[t][:, :S], -2.0, h12[:], ALU.mult, ALU.add)
+            else:
+                nc.vector.tensor_tensor(part[:, t, :], hop1[t][:].indirect(n2_t[:]), minus_2y[t][:], ALU.add)
+            nc.scalar.activation(scaled[:, t, :], hop1[t][:, :S], ACT.Copy, scale=unit_t[:, t : t + 1])
+            nc.scalar.activation(h13[:, t, :], hop1[t][:].indirect(entries(n3_t, HALF, HALF)), ACT.Copy)
+            nc.vector.tensor_tensor(
+                arg_left[:, t, :], hop1[t][:].indirect(entries(n3_t, 0, HALF)), part[:, t, :HALF], ALU.add
+            )
 
         out_words = sb([P, S], U32, "out_words")
         out_scales = sb([P, S], U8, "out_scales")
@@ -174,46 +174,48 @@ def tile_picked_ytwohop_mul_po_kernel(
 
         for c in range(CHUNKS):
             cols = slice(c * CHUNK, (c + 1) * CHUNK)
-            h13 = sb([P, LATE, CHUNK], F32, f"h13_{c}")
-            arg = sb([P, LATE, CHUNK], F32, f"arg_late{c}")
-            gate = sb([P, LATE, CHUNK], F32, f"gate_late{c}")
-            for u in range(LATE):
-                nc.scalar.activation(
-                    h13[:, u, :], hop1[EARLY + u][:].indirect(entries(n3_t, c * CHUNK, CHUNK)), ACT.Copy
-                )
-            nc.vector.tensor_tensor(arg[:], h13[:], part_late[:, :, cols], ALU.add)
-            nc.scalar.activation(gate[:], arg[:], ACT.Tanh, scale=0.6)
-            for u in range(LATE):
-                hidden(EARLY + u, cols, gate[:, u, :])
+            gate = sb([P, PACK, CHUNK], F32, f"gate{c}")
+            if cols.stop <= HALF:
+                arg = arg_left[:, :, cols]
+            else:
+                arg = sb([P, PACK, CHUNK], F32, f"arg{c}")[:]
+                nc.vector.tensor_tensor(arg, h13[:, :, cols.start - HALF : cols.stop - HALF], part[:, :, cols], ALU.add)
+            nc.scalar.activation(gate[:], arg, ACT.Tanh, scale=0.6)
 
             hid_woven = sb([P, CHUNK, PACK], BF16, f"hid_woven{c}")
             hid_words = sb([P, CHUNK], U32, f"hid_words{c}")
             hid_scales = sb([P, CHUNK], U8, f"hid_scales{c}")
-            if c < SCALAR_WEAVES:
-                nc.scalar.copy(woven(hid_woven[:]), planes(hid[:, :, cols]))
-            else:
-                nc.vector.tensor_copy(woven(hid_woven[:]), planes(hid[:, :, cols]))
+            nc.vector.tensor_tensor(woven(hid_woven[:]), planes(scaled[:, :, cols]), planes(gate[:]), ALU.mult)
             nc.vector.quantize_mx(hid_words[:].bitcast(FP8X4), hid_scales[:], hid_woven[:].rearrange("p c t -> p (c t)"))
 
-            acc = psum.tile([P, PACK, CHUNK], F32, name=f"out_acc{c}", tag="bank")
-            for t in range(PACK):
-                nc.tensor.matmul_mx(
-                    acc[:, t, :],
-                    lhsT=w2w[:, 2 * P * t : 2 * P * (t + 1)].bitcast(FP4X4),
-                    lhsT_scale=w2s[:, P * t : P * (t + 1)],
-                    rhs=hid_words[:].bitcast(FP8X4),
-                    rhs_scale=hid_scales[:],
-                    start=True,
-                    stop=True,
-                )
+            def second_product(first, count):
+                acc = psum.tile([P, count, CHUNK], F32, name=f"out_acc{c}_{first}", tag="bank")
+                for u in range(count):
+                    t = first + u
+                    nc.tensor.matmul_mx(
+                        acc[:, u, :],
+                        lhsT=w2w[:, 2 * P * t : 2 * P * (t + 1)].bitcast(FP4X4),
+                        lhsT_scale=w2s[:, P * t : P * (t + 1)],
+                        rhs=hid_words[:].bitcast(FP8X4),
+                        rhs_scale=hid_scales[:],
+                        start=True,
+                        stop=True,
+                    )
+                return acc
+
             res = sb([P, PACK, CHUNK], F32, f"res{c}")
             res_woven = sb([P, CHUNK, PACK], BF16, f"res_woven{c}")
-            if c < CHUNKS - 1:
-                nc.scalar.copy(res[:], acc[:])
+            if c == CHUNKS - 1:
+                nc.scalar.copy(res[:, : PACK // 2, :], second_product(0, PACK // 2)[:])
+                nc.vector.tensor_copy(res[:, PACK // 2 :, :], second_product(PACK // 2, PACK // 2)[:])
+                nc.vector.tensor_copy(woven(res_woven[:]), planes(res[:]))
+            elif c < VECTOR_WEAVES:
+                nc.scalar.copy(res[:], second_product(0, PACK)[:])
                 nc.vector.tensor_copy(woven(res_woven[:]), planes(res[:]))
             else:
+                acc = second_product(0, PACK)
                 nc.scalar.copy(res_woven[:], acc[:].rearrange("p t c -> p c t"))
-                nc.vector.tensor_copy(res[:], acc[:])
+                nc.scalar.copy(res[:], acc[:])
             nc.sync.dma_start(out_rows[:, :, cols], res[:])
             nc.vector.quantize_mx(
                 out_words[:, cols].bitcast(FP8X4), out_scales[:, cols], res_woven[:].rearrange("p c t -> p (c t)")

@@ -22,11 +22,11 @@ QUADS = 4
 PASSES = K // (P * PACK)
 GROUP = 16
 HALF = S // 2
-Y_SPARE = 192
-HOP_SPARE = 16
+SPARE = 16
 CHUNK = 128
 CHUNKS = S // CHUNK
-SCALAR_SECOND = 2
+SHARED_TILES = 2
+SCALAR_SECOND = 3
 VECTOR_WEAVES = 2
 
 
@@ -49,13 +49,13 @@ def tile_picked_ytwohop_mul_po_kernel(
         xw_raw = [sb([P, T], I32, f"xw_raw{o}") for o in range(PASSES)]
         w1w_raw = sb([P, PASSES, 2 * H], U8, "w1w_raw")
         w1s_raw = sb([P, PASSES, H], U8, "w1s_raw")
+        w2w_raw = sb([P, 2 * N], U8, "w2w_raw")
         w2s_raw = sb([P, 1, N], U8, "w2s_raw")
         unit_t = sb([P, PACK], F32, "unit_t")
-        y = [sb([P, S + Y_SPARE], F32, f"y{t}") for t in range(PACK)]
-        hop1 = [sb([P, S + HOP_SPARE], F32, f"hop1_{t}") for t in range(PACK)]
+        y = [sb([P, S + SPARE], F32, f"y{t}") for t in range(PACK)]
+        hop1 = [sb([P, S + SPARE], F32, f"hop1_{t}") for t in range(PACK)]
 
-        nc.gpsimd.memset(xs_raw[:, 0, :].bitcast(I32), 0)
-        nc.vector.memset(xs_raw[:, 1, :].bitcast(I32), 0)
+        nc.gpsimd.memset(xs_raw[:].rearrange("p o c -> p (o c)").bitcast(I32), 0)
         nc.vector.memset(w1s_raw[:].rearrange("p o c -> p (o c)").bitcast(I32), 0)
         nc.vector.memset(w2s_raw[:, 0, :].bitcast(I32), 0)
         for window in y + hop1:
@@ -68,46 +68,44 @@ def tile_picked_ytwohop_mul_po_kernel(
                     src[:, 4 * q : 4 * q + 4, :].rearrange("o r c -> r o c").bitcast(I32),
                 )
 
-        def load_x_words(queue, o):
-            queue.dma_start(xw_raw[o][:], x_words[o].rearrange("p c r -> p (c r)").bitcast(I32))
+        def load_x_words(o):
+            nc.sync.dma_start(xw_raw[o][:], x_words[o].rearrange("p c r -> p (c r)").bitcast(I32))
 
         nc.sync.dma_start(offs_t[:], offs)
-        load_x_words(nc.scalar, 0)
-        nc.scalar.dma_start(w1w_raw[:].bitcast(I32), w1_words.rearrange("o p c -> p o c").bitcast(I32))
         load_scales(xs_raw, x_scales)
         nc.sync.dma_start(n1_t[:], n1)
-        load_scales(w1s_raw, w1_scales)
-        load_x_words(nc.sync, 1)
         nc.sync.dma_start(n2_t[:], n2)
+        load_x_words(0)
+        nc.sync.dma_start(w1w_raw[:].bitcast(I32), w1_words.rearrange("o p c -> p o c").bitcast(I32))
+        load_scales(w1s_raw, w1_scales)
+        load_x_words(1)
         nc.sync.dma_start(n3_t[:], n3)
         load_scales(w2s_raw, w2_scales)
-        nc.gpsimd.dma_start(unit_t[:], unit.rearrange("(p t) one -> p (t one)", t=PACK))
+        nc.sync.dma_start(w2w_raw[:].bitcast(I32), w2_words[0].bitcast(I32))
+        nc.sync.dma_start(unit_t[:], unit.rearrange("(p t) one -> p (t one)", t=PACK))
 
         halves = [slice(0, HALF), slice(HALF, S)]
         xs = [sb([P, S], U8, f"xs{o}") for o in range(PASSES)]
         xw = [sb([P, S], U32, f"xw{o}") for o in range(PASSES)]
-        nc.vector.tensor_copy(xw[0][:], xw_raw[0][:].bitcast(U32).indirect(offs_t[:]))
         for o in range(PASSES):
             nc.vector.tensor_copy(xs[o][:], xs_raw[:, o, :].indirect(offs_t[:]))
+        nc.vector.tensor_copy(xw[0][:], xw_raw[0][:].bitcast(U32).indirect(offs_t[:]))
         for cols in halves:
             nc.vector.tensor_copy(xw[1][:, cols], xw_raw[1][:].bitcast(U32).indirect(entries(offs_t, cols.start, HALF)))
 
-        w1w = [sb([P, 2 * H], U8, f"w1w{o}") for o in range(PASSES)]
-        w1s = [[sb([P, P], U8, f"w1s{o}_{t}") for t in range(PACK)] for o in range(PASSES)]
+        w1w = sb([P, PASSES, 2 * H], U8, "w1w")
+        w1s = [sb([P, PASSES, P], U8, f"w1s{t}") for t in range(PACK)]
         w2w = sb([P, 2 * N], U8, "w2w")
         w2s = sb([P, N], U8, "w2s")
-        for o in range(PASSES):
-            nc.scalar.copy(
-                w1w[o][:].bitcast(U16).rearrange("p (t m) -> p t m", t=PACK),
-                w1w_raw[:, o, :].bitcast(U16).rearrange("p (m t) -> p t m", t=PACK),
-            )
-            for t in range(PACK):
-                nc.gpsimd.tensor_copy(w1s[o][t][:], w1s_raw[:, o, :].rearrange("p (m t) -> p t m", t=PACK)[:, t])
-        w2w_raw = w1w_raw[:, 0, :]
-        nc.sync.dma_start(w2w_raw.bitcast(I32), w2_words[0].bitcast(I32))
+        nc.scalar.copy(
+            w1w[:].bitcast(U16).rearrange("p o (t m) -> p o t m", t=PACK),
+            w1w_raw[:].bitcast(U16).rearrange("p o (m t) -> p o t m", t=PACK),
+        )
+        for t in range(PACK):
+            nc.gpsimd.tensor_copy(w1s[t][:], w1s_raw[:].rearrange("p o (m t) -> p t o m", t=PACK)[:, t])
         nc.scalar.copy(
             w2w[:].bitcast(U16).rearrange("p (t m) -> p t m", t=PACK),
-            w2w_raw.bitcast(U16).rearrange("p (m t) -> p t m", t=PACK),
+            w2w_raw[:].bitcast(U16).rearrange("p (m t) -> p t m", t=PACK),
         )
         nc.gpsimd.tensor_copy(w2s[:].rearrange("p (t m) -> p t m", t=PACK), w2s_raw[:, 0, :].rearrange("p (m t) -> p t m", t=PACK))
 
@@ -117,8 +115,8 @@ def tile_picked_ytwohop_mul_po_kernel(
                 for h, cols in enumerate(halves):
                     nc.tensor.matmul_mx(
                         y_acc[t][h][:],
-                        lhsT=w1w[o][:, 2 * P * t : 2 * P * (t + 1)].bitcast(FP4X4),
-                        lhsT_scale=w1s[o][t][:],
+                        lhsT=w1w[:, o, 2 * P * t : 2 * P * (t + 1)].bitcast(FP4X4),
+                        lhsT_scale=w1s[t][:, o, :],
                         rhs=xw[o][:, cols].bitcast(FP8X4),
                         rhs_scale=xs[o][:, cols],
                         start=(o == 0),
@@ -126,7 +124,7 @@ def tile_picked_ytwohop_mul_po_kernel(
                     )
         for t in range(PACK):
             for h, cols in enumerate(halves):
-                if t == 0 and h == 1:
+                if t < SHARED_TILES and h == 1:
                     nc.vector.tensor_copy(y[t][:, cols], y_acc[t][h][:])
                 else:
                     nc.scalar.copy(y[t][:, cols], y_acc[t][h][:])
@@ -134,7 +132,7 @@ def tile_picked_ytwohop_mul_po_kernel(
         minus_2y = {}
         for t in range(PACK):
             y1 = sb([P, S], F32, f"y1_{t}")
-            if t == 0:
+            if t < SHARED_TILES:
                 nc.vector.tensor_copy(y1[:, :HALF], y[t][:].indirect(entries(n1_t, 0, HALF)))
                 nc.scalar.activation(y1[:, HALF:], y[t][:].indirect(entries(n1_t, HALF, HALF)), ACT.Copy)
             else:
@@ -155,7 +153,10 @@ def tile_picked_ytwohop_mul_po_kernel(
                 nc.vector.scalar_tensor_tensor(part[:, t, :], y[t][:, :S], -2.0, h12[:], ALU.mult, ALU.add)
             else:
                 nc.vector.tensor_tensor(part[:, t, :], hop1[t][:].indirect(n2_t[:]), minus_2y[t][:], ALU.add)
-            nc.scalar.activation(scaled[:, t, :], hop1[t][:, :S], ACT.Copy, scale=unit_t[:, t : t + 1])
+            if t < SHARED_TILES:
+                nc.vector.tensor_scalar(scaled[:, t, :], hop1[t][:, :S], unit_t[:, t : t + 1], None, ALU.mult)
+            else:
+                nc.scalar.activation(scaled[:, t, :], hop1[t][:, :S], ACT.Copy, scale=unit_t[:, t : t + 1])
             nc.scalar.activation(h13[:, t, :], hop1[t][:].indirect(entries(n3_t, HALF, HALF)), ACT.Copy)
             nc.vector.tensor_tensor(
                 arg_left[:, t, :], hop1[t][:].indirect(entries(n3_t, 0, HALF)), part[:, t, :HALF], ALU.add

from contextlib import ExitStack

import concourse.mybir as mybir

K, T, S, N, H = 1024, 1024, 512, 512, 512
FLOPS = 2 * K * H * S + 2 * H * N * S

F32 = mybir.dt.float32
BF16 = mybir.dt.bfloat16
I32 = mybir.dt.int32
U32 = mybir.dt.uint32
U16 = mybir.dt.uint16
U8 = mybir.dt.uint8
FP8X4 = mybir.dt.float8_e4m3fn_x4
FP4X4 = mybir.dt.float4_e2m1fn_x4
ACT = mybir.ActivationFunctionType
ALU = mybir.AluOpType

P = 128
PACK = 4
QUADS = 4
PASSES = K // (P * PACK)
GROUP = 16
HALF = S // 2
SPARE = 16
CHUNK = 128
CHUNKS = S // CHUNK
SHARED_TILES = 2
SCALAR_SECOND = 3
VECTOR_WEAVES = 2


def tile_picked_ytwohop_mul_po_kernel(
    tc, x_words, x_scales, w1_words, w1_scales, unit, w2_words, w2_scales, offs, n1, n2, n3, out_0, out_1, out_2
):
    nc = tc.nc
    with ExitStack() as ctx:
        keep = ctx.enter_context(tc.tile_pool(name="keep", bufs=1))
        psum = ctx.enter_context(tc.psum_pool(name="psum", bufs=8))

        def sb(shape, dtype, name):
            return keep.tile(shape, dtype, name=name, align_bytes=64)

        def entries(lst, start, count):
            return lst[:, start // GROUP : (start + count) // GROUP]

        offs_t, n1_t, n2_t, n3_t = [sb([P, S // GROUP], U16, name) for name in ("offs_t", "n1_t", "n2_t", "n3_t")]
        xs_raw = sb([P, PASSES, T], U8, "xs_raw")
        xw_raw = [sb([P, T], I32, f"xw_raw{o}") for o in range(PASSES)]
        w1w_raw = sb([P, PASSES, 2 * H], U8, "w1w_raw")
        w1s_raw = sb([P, PASSES, H], U8, "w1s_raw")
        w2w_raw = sb([P, 2 * N], U8, "w2w_raw")
        w2s_raw = sb([P, 1, N], U8, "w2s_raw")
        unit_t = sb([P, PACK], F32, "unit_t")
        y = [sb([P, S + SPARE], F32, f"y{t}") for t in range(PACK)]
        hop1 = [sb([P, S + SPARE], F32, f"hop1_{t}") for t in range(PACK)]

        nc.gpsimd.memset(xs_raw[:].rearrange("p o c -> p (o c)").bitcast(I32), 0)
        nc.vector.memset(w1s_raw[:].rearrange("p o c -> p (o c)").bitcast(I32), 0)
        nc.vector.memset(w2s_raw[:, 0, :].bitcast(I32), 0)
        for window in y + hop1:
            nc.vector.memset(window[:, S:], 0.0)

        def load_scales(dst, src):
            for q in range(QUADS):
                nc.sync.dma_start(
                    dst[32 * q : 32 * q + 4, :, :].bitcast(I32),
                    src[:, 4 * q : 4 * q + 4, :].rearrange("o r c -> r o c").bitcast(I32),
                )

        def load_x_words(o):
            nc.sync.dma_start(xw_raw[o][:], x_words[o].rearrange("p c r -> p (c r)").bitcast(I32))

        nc.sync.dma_start(offs_t[:], offs)
        load_scales(xs_raw, x_scales)
        nc.sync.dma_start(n1_t[:], n1)
        nc.sync.dma_start(n2_t[:], n2)
        load_x_words(0)
        nc.sync.dma_start(w1w_raw[:].bitcast(I32), w1_words.rearrange("o p c -> p o c").bitcast(I32))
        load_scales(w1s_raw, w1_scales)
        load_x_words(1)
        nc.sync.dma_start(n3_t[:], n3)
        load_scales(w2s_raw, w2_scales)
        nc.sync.dma_start(w2w_raw[:].bitcast(I32), w2_words[0].bitcast(I32))
        nc.sync.dma_start(unit_t[:], unit.rearrange("(p t) one -> p (t one)", t=PACK))

        halves = [slice(0, HALF), slice(HALF, S)]
        xs = [sb([P, S], U8, f"xs{o}") for o in range(PASSES)]
        xw = [sb([P, S], U32, f"xw{o}") for o in range(PASSES)]
        for o in range(PASSES):
            nc.vector.tensor_copy(xs[o][:], xs_raw[:, o, :].indirect(offs_t[:]))
        nc.vector.tensor_copy(xw[0][:], xw_raw[0][:].bitcast(U32).indirect(offs_t[:]))
        for cols in halves:
            nc.vector.tensor_copy(xw[1][:, cols], xw_raw[1][:].bitcast(U32).indirect(entries(offs_t, cols.start, HALF)))

        w1w = sb([P, PASSES, 2 * H], U8, "w1w")
        w1s = [sb([P, PASSES, P], U8, f"w1s{t}") for t in range(PACK)]
        w2w = sb([P, 2 * N], U8, "w2w")
        w2s = sb([P, N], U8, "w2s")
        nc.scalar.copy(
            w1w[:].bitcast(U16).rearrange("p o (t m) -> p o t m", t=PACK),
            w1w_raw[:].bitcast(U16).rearrange("p o (m t) -> p o t m", t=PACK),
        )
        for t in range(PACK):
            nc.gpsimd.tensor_copy(w1s[t][:], w1s_raw[:].rearrange("p o (m t) -> p t o m", t=PACK)[:, t])
        nc.scalar.copy(
            w2w[:].bitcast(U16).rearrange("p (t m) -> p t m", t=PACK),
            w2w_raw[:].bitcast(U16).rearrange("p (m t) -> p t m", t=PACK),
        )
        nc.gpsimd.tensor_copy(w2s[:].rearrange("p (t m) -> p t m", t=PACK), w2s_raw[:, 0, :].rearrange("p (m t) -> p t m", t=PACK))

        y_acc = [[psum.tile([P, HALF], F32, name=f"y_acc{t}_{h}", tag="bank") for h in range(2)] for t in range(PACK)]
        for t in range(PACK):
            for o in range(PASSES):
                for h, cols in enumerate(halves):
                    nc.tensor.matmul_mx(
                        y_acc[t][h][:],
                        lhsT=w1w[:, o, 2 * P * t : 2 * P * (t + 1)].bitcast(FP4X4),
                        lhsT_scale=w1s[t][:, o, :],
                        rhs=xw[o][:, cols].bitcast(FP8X4),
                        rhs_scale=xs[o][:, cols],
                        start=(o == 0),
                        stop=(o == PASSES - 1),
                    )
        for t in range(PACK):
            for h, cols in enumerate(halves):
                if t < SHARED_TILES and h == 1:
                    nc.vector.tensor_copy(y[t][:, cols], y_acc[t][h][:])
                else:
                    nc.scalar.copy(y[t][:, cols], y_acc[t][h][:])

        minus_2y = {}
        for t in range(PACK):
            y1 = sb([P, S], F32, f"y1_{t}")
            if t < SHARED_TILES:
                nc.vector.tensor_copy(y1[:, :HALF], y[t][:].indirect(entries(n1_t, 0, HALF)))
                nc.scalar.activation(y1[:, HALF:], y[t][:].indirect(entries(n1_t, HALF, HALF)), ACT.Copy)
            else:
                nc.scalar.activation(y1[:], y[t][:].indirect(n1_t[:]), ACT.Copy)
            nc.vector.tensor_tensor(hop1[t][:, :S], y[t][:].indirect(n2_t[:]), y1[:], ALU.add)
            if t >= SCALAR_SECOND:
                minus_2y[t] = sb([P, S], F32, f"minus_2y{t}")
                nc.vector.tensor_scalar(minus_2y[t][:], y[t][:, :S], -2.0, None, ALU.mult)

        part = sb([P, PACK, S], F32, "part")
        scaled = sb([P, PACK, S], F32, "scaled")
        h13 = sb([P, PACK, HALF], F32, "h13")
        arg_left = sb([P, PACK, HALF], F32, "arg_left")
        for t in range(PACK):
            if t < SCALAR_SECOND:
                h12 = sb([P, S], F32, f"h12_{t}")
                nc.scalar.activation(h12[:], hop1[t][:].indirect(n2_t[:]), ACT.Copy)
                nc.vector.scalar_tensor_tensor(part[:, t, :], y[t][:, :S], -2.0, h12[:], ALU.mult, ALU.add)
            else:
                nc.vector.tensor_tensor(part[:, t, :], hop1[t][:].indirect(n2_t[:]), minus_2y[t][:], ALU.add)
            if t < SHARED_TILES:
                nc.vector.tensor_scalar(scaled[:, t, :], hop1[t][:, :S], unit_t[:, t : t + 1], None, ALU.mult)
            else:
                nc.scalar.activation(scaled[:, t, :], hop1[t][:, :S], ACT.Copy, scale=unit_t[:, t : t + 1])
            nc.scalar.activation(h13[:, t, :], hop1[t][:].indirect(entries(n3_t, HALF, HALF)), ACT.Copy)
            nc.vector.tensor_tensor(
                arg_left[:, t, :], hop1[t][:].indirect(entries(n3_t, 0, HALF)), part[:, t, :HALF], ALU.add
            )

        out_words = sb([P, S], U32, "out_words")
        out_scales = sb([P, S], U8, "out_scales")
        out_rows = out_0.rearrange("(p t) j -> p t j", t=PACK)
        out_words_dram = out_1[0].rearrange("p c r -> p (c r)").bitcast(I32)

        def woven(tile):
            return tile.rearrange("p (c i) t -> p c t i", i=4)

        def planes(tile):
            return tile.rearrange("p t (c i) -> p c t i", i=4)

        for c in range(CHUNKS):
            cols = slice(c * CHUNK, (c + 1) * CHUNK)
            gate = sb([P, PACK, CHUNK], F32, f"gate{c}")
            if cols.stop <= HALF:
                arg = arg_left[:, :, cols]
            else:
                arg = sb([P, PACK, CHUNK], F32, f"arg{c}")[:]
                nc.vector.tensor_tensor(arg, h13[:, :, cols.start - HALF : cols.stop - HALF], part[:, :, cols], ALU.add)
            nc.scalar.activation(gate[:], arg, ACT.Tanh, scale=0.6)

            hid_woven = sb([P, CHUNK, PACK], BF16, f"hid_woven{c}")
            hid_words = sb([P, CHUNK], U32, f"hid_words{c}")
            hid_scales = sb([P, CHUNK], U8, f"hid_scales{c}")
            nc.vector.tensor_tensor(woven(hid_woven[:]), planes(scaled[:, :, cols]), planes(gate[:]), ALU.mult)
            nc.vector.quantize_mx(hid_words[:].bitcast(FP8X4), hid_scales[:], hid_woven[:].rearrange("p c t -> p (c t)"))

            def second_product(first, count):
                acc = psum.tile([P, count, CHUNK], F32, name=f"out_acc{c}_{first}", tag="bank")
                for u in range(count):
                    t = first + u
                    nc.tensor.matmul_mx(
                        acc[:, u, :],
                        lhsT=w2w[:, 2 * P * t : 2 * P * (t + 1)].bitcast(FP4X4),
                        lhsT_scale=w2s[:, P * t : P * (t + 1)],
                        rhs=hid_words[:].bitcast(FP8X4),
                        rhs_scale=hid_scales[:],
                        start=True,
                        stop=True,
                    )
                return acc

            res = sb([P, PACK, CHUNK], F32, f"res{c}")
            res_woven = sb([P, CHUNK, PACK], BF16, f"res_woven{c}")
            if c == CHUNKS - 1:
                nc.scalar.copy(res[:, : PACK // 2, :], second_product(0, PACK // 2)[:])
                nc.vector.tensor_copy(res[:, PACK // 2 :, :], second_product(PACK // 2, PACK // 2)[:])
                nc.vector.tensor_copy(woven(res_woven[:]), planes(res[:]))
            elif c < VECTOR_WEAVES:
                nc.scalar.copy(res[:], second_product(0, PACK)[:])
                nc.vector.tensor_copy(woven(res_woven[:]), planes(res[:]))
            else:
                acc = second_product(0, PACK)
                nc.scalar.copy(res_woven[:], acc[:].rearrange("p t c -> p c t"))
                nc.scalar.copy(res[:], acc[:])
            nc.sync.dma_start(out_rows[:, :, cols], res[:])
            nc.vector.quantize_mx(
                out_words[:, cols].bitcast(FP8X4), out_scales[:, cols], res_woven[:].rearrange("p c t -> p (c t)")
            )
            nc.sync.dma_start(out_words_dram[:, cols], out_words[:, cols].bitcast(I32))
        for q in range(QUADS):
            queue = nc.sync if q % 2 == 0 else nc.scalar
            queue.dma_start(out_2[0, 4 * q : 4 * q + 4, :].bitcast(I32), out_scales[32 * q : 32 * q + 4, :].bitcast(I32))
